import numpy as np
import ml_dtypes


def mxq(x, axis, fmt="e4m3"):
    dtype, down = {"e4m3": (ml_dtypes.float8_e4m3fn, 7), "e5m2": (ml_dtypes.float8_e5m2, 14)}[fmt]
    v = np.moveaxis(np.asarray(x, np.float32).astype(ml_dtypes.bfloat16).astype(np.float64), axis, -1)
    blocks = v.reshape(v.shape[:-1] + (-1, 32))
    amax = np.abs(blocks).max(-1, keepdims=True)
    byte = np.maximum(np.where(amax > 0, np.frexp(amax)[1] - 1 + 127, 0) - down, 1)
    scale = np.exp2(byte - 127.0)
    codes = (blocks / scale).astype(np.float32).astype(dtype).astype(np.float64)
    return np.moveaxis((codes * scale).reshape(v.shape), -1, axis)


WIDE = False


def mx_kscale(k):
    if not WIDE:
        return np.ones(k)
    levels = np.array([18, -18])
    if k % 512:
        return np.exp2(np.random.permutation(np.resize(levels, k // 32))).repeat(32)
    a = np.empty((k // 512, 16))
    for p in range(k // 512):
        a[p, :8] = np.random.permutation(np.resize(levels, 8))
        for g in range(8):
            far = levels[np.abs(levels - a[p, g]) >= 10]
            a[p, g + 8] = far[np.random.randint(len(far))]
    return np.exp2(a.ravel()).repeat(32)


def f64(x):
    return np.asarray(x).astype(np.float64)


def striped(idx):
    return np.tile(np.asarray(idx).reshape(-1, 16).T, (8, 1)).astype(np.uint16)


def unstriped(offs):
    return offs[:16].T.reshape(-1).astype(np.int64)

def planes(y):
    n, m = y.shape
    v = y.astype(np.float32).astype(ml_dtypes.bfloat16).astype(np.float64).reshape(n // 32, 32, m)
    top = np.abs(v).max(1)
    byte = np.clip(np.where(top > 0, np.frexp(top)[1] - 1 + 127 - 7, 1), 1, 254)
    codes = (v * np.exp2(127.0 - byte)[:, None, :]).reshape(n, m).astype(np.float32).astype(ml_dtypes.float8_e4m3fn).view(np.uint8)
    words = codes.reshape(n // 512, 128, 4, m).transpose(0, 1, 3, 2)
    return np.ascontiguousarray(words), np.ascontiguousarray(byte.astype(np.uint8).reshape(n // 512, 16, m))


B, N, T, D, R = 1, 512, 2048, 512, 1024


def setup_inputs():
    n = np.random.standard_normal
    idx = np.random.permutation(T)[:B * N]
    s = mx_kscale(D)[:, None]
    u = np.ones(T)
    u[idx] = mx_kscale(B * N)
    r = np.random.uniform(0.5, 2.0, T) * u
    x = n((B, D, R))
    return {
        "xT": (x * s).astype(np.float32),
        "wT": (n((D, T)) * (1.00 / np.sqrt(D)) / s / r).astype(np.float32),
        "y": n((B, R, N)).astype(np.float32),
        "wt": (np.random.uniform(0.5, 1.5, (B, R, 1)) * 1.0 / np.sqrt(R)).astype(np.float32),
        "ts": np.tile(r, (128, 1)).astype(np.float32),
        "offs": striped(idx),
    }


def reference(xT, wT, y, wt, ts, offs):
    idx = unstriped(offs)
    pick = lambda x: x[:, idx].reshape(x.shape[0], B, N).transpose(1, 0, 2)
    w = pick(f64(wT))
    a = mxq(f64(xT), 1, "e4m3").transpose(0, 2, 1) @ mxq(w, 1, "e4m3")
    ts_ = pick(f64(ts))[:, :1, :]
    a = a * ts_
    g = f64(wt) * np.minimum(np.maximum(a - f64(y), -1.0), 1.0)
    g = g * ts_
    gx = mxq(g, 2, "e5m2") @ mxq(w, 2, "e4m3").transpose(0, 2, 1)
    out_0 = gx
    return (out_0,) + planes(out_0[0])

@@ -1,0 +1,229 @@
+from contextlib import ExitStack
+
+import concourse.mybir as mybir
+from concourse.masks import make_identity
+
+F32 = mybir.dt.float32
+BF16 = mybir.dt.bfloat16
+I32 = mybir.dt.int32
+U32 = mybir.dt.uint32
+U16 = mybir.dt.uint16
+U8 = mybir.dt.uint8
+E4M3 = mybir.dt.float8_e4m3fn_x4
+E5M2 = mybir.dt.float8_e5m2_x4
+ALU = mybir.AluOpType
+COPY = mybir.ActivationFunctionType.Copy
+
+P = 128
+PACK = 4
+SLOTS, ITEMS, D, R = 512, 2048, 512, 1024
+PASS = P * PACK
+GROUPS = R // PASS
+PAIR = 2
+UNIT = PAIR * P
+FLOPS = 2 * 2 * R * SLOTS * D
+
+
+def tile_attend_ghub_pl_x_ts_kernel(tc, xT, wT, y, wt, ts, offs, out_0, out_1, out_2):
+    nc = tc.nc
+    units = [(o, f) for o in range(GROUPS) for f in range(PACK // PAIR)]
+
+    with ExitStack() as ctx:
+        held = ctx.enter_context(tc.tile_pool(name="held", bufs=1))
+        psum = ctx.enter_context(tc.psum_pool(name="psum", bufs=2))
+
+        def sb(name, shape, dtype):
+            return held.tile(shape, dtype, name=name, align_bytes=64)
+
+        offsets = held.tile([P, SLOTS // 16], U16, name="offsets")
+        table = [sb("table%d" % t, [P, ITEMS], F32) for t in range(PACK)]
+        ts_row = sb("ts_row", [P, ITEMS], F32)
+        wt_col = sb("wt_col", [P, GROUPS, PACK], F32)
+        x_raw = [sb("x_raw%d" % o, [P, PACK, PASS], F32) for o in range(GROUPS)]
+        y_raw = {u: sb("y_raw%d%d" % u, [P, PAIR, SLOTS], F32) for u in units}
+
+        w_planes = wT.rearrange("(p t) n -> t p n", t=PACK)
+        x_view = xT[0].rearrange("(p j) r -> p j r", j=PACK)
+        y_view = y[0].rearrange("(o p t) i -> o p t i", p=P, t=PACK)
+        out_view = out_0[0].rearrange("(o p t) d -> o p t d", p=P, t=PACK)
+
+        nc.sync.dma_start(table[0][:], w_planes[0])
+        nc.vector.memset(ts_row[:], 0.0)
+        nc.sync.dma_start(ts_row[0:1, :], ts[0:1, :])
+        nc.sync.dma_start(offsets[:], offs)
+        nc.scalar.dma_start(wt_col[:], wt[0].rearrange("(o p t) one -> p o (t one)", p=P, t=PACK))
+        nc.sync.dma_start(x_raw[0][:], x_view[:, :, :PASS])
+        for t in range(1, PACK):
+            nc.sync.dma_start(table[t][:], w_planes[t])
+        for o in range(GROUPS):
+            if o > 0:
+                nc.sync.dma_start(x_raw[o][:], x_view[:, :, o * PASS : (o + 1) * PASS])
+            for f in range(PACK // PAIR):
+                nc.sync.dma_start(y_raw[o, f][:], y_view[o][:, PAIR * f : PAIR * (f + 1), :])
+
+        ident = sb("ident", [P, P], F32)
+        make_identity(nc, ident[:])
+
+        ts_listed = sb("ts_listed", [P, SLOTS], F32)
+        nc.scalar.activation(ts_listed[:], ts_row[:].indirect(offsets[:]), COPY)
+        ts_bank = psum.tile([P, PACK, P], F32, tag="acc", name="ts_bank")
+        for t in range(PACK):
+            nc.tensor.transpose(ts_bank[:, t, :], ts_listed[:, t::PACK], ident[:])
+        ts_col = sb("ts_col", [P, PACK], F32)
+        ts_sq = sb("ts_sq", [P, PACK], F32)
+        ts_neg = sb("ts_neg", [P, PACK], F32)
+        hi = sb("hi", [P, PACK], F32)
+        lo = sb("lo", [P, PACK], F32)
+        nc.vector.tensor_copy(ts_col[:], ts_bank[:, :, 0])
+        nc.vector.tensor_tensor(ts_sq[:], ts_col[:], ts_col[:], ALU.mult)
+        nc.vector.tensor_scalar(ts_neg[:], ts_col[:], -1.0, None, ALU.mult)
+        nc.vector.tensor_tensor(hi[:], ts_col[:], ts_neg[:], ALU.max)
+        nc.vector.tensor_tensor(lo[:], ts_col[:], ts_neg[:], ALU.min)
+
+        wt_bank = []
+        for o in range(GROUPS):
+            bank = psum.tile([P, PACK, P], F32, tag="wt", name="wt_bank%d" % o)
+            for t in range(PACK):
+                nc.tensor.transpose(bank[:, t, :], wt_col[:, o, t : t + 1].to_broadcast([P, P]), ident[:])
+            wt_bank.append(bank)
+
+        x_codes, x_scales, y_scaled, clipped = {}, {}, {}, {}
+        out_sb = [sb("out_sb%d" % o, [P, PACK, D], F32) for o in range(GROUPS)]
+
+        def prepare_x(u, copy):
+            o, f = u
+            x_in = sb("x_in%d%d" % u, [P, P, PAIR, PACK], BF16)
+            src = x_raw[o][:].rearrange("p j (m f e) -> p f m j e", f=PACK // PAIR, e=PAIR)[:, f]
+            copy(x_in[:].rearrange("p m e j -> p m j e"), src)
+            x_codes[u] = sb("x_codes%d%d" % u, [P, UNIT], U32)
+            x_scales[u] = sb("x_scales%d%d" % u, [P, UNIT], U8)
+            nc.vector.quantize_mx(x_codes[u][:].bitcast(E4M3), x_scales[u][:], x_in[:].rearrange("p m e j -> p (m e j)"))
+
+        def turn_y(u):
+            y_scaled[u] = sb("y_scaled%d%d" % u, [P, PACK, UNIT], F32)
+            for b in range(2):
+                bank = psum.tile([P, 2, PAIR, P], F32, tag="yt", name="y_bank")
+                for k in range(2):
+                    for e in range(PAIR):
+                        nc.tensor.transpose(bank[:, k, e, :], y_raw[u][:, e, 2 * b + k :: PACK], ident[:])
+                for k in range(2):
+                    t = 2 * b + k
+                    nc.scalar.activation(
+                        y_scaled[u][:, t, :], bank[:, k].rearrange("p e m -> p (e m)"), COPY, scale=ts_col[:, t : t + 1]
+                    )
+
+        def scores(u):
+            diff = sb("diff%d%d" % u, [P, PACK, UNIT], F32)
+            clipped[u] = sb("clipped%d%d" % u, [P, PACK, UNIT], F32)
+            for b in range(2):
+                bank = psum.tile([P, 2, UNIT], F32, tag="sc", name="s_bank")
+                for k in range(2):
+                    cols = slice((2 * b + k) * P, (2 * b + k + 1) * P)
+                    nc.tensor.matmul_mx(
+                        bank[:, k, :], wd_codes[:, cols].bitcast(E4M3), wd_scales[:, cols],
+                        x_codes[u][:].bitcast(E4M3), x_scales[u][:], start=True, stop=True,
+                    )
+                for k in range(2):
+                    t = 2 * b + k
+                    nc.vector.scalar_tensor_tensor(
+                        diff[:, t, :].rearrange("p (e m) -> p e m", e=PAIR),
+                        bank[:, k, :].rearrange("p (m e) -> p e m", e=PAIR),
+                        ts_sq[:, t : t + 1],
+                        y_scaled[u][:, t, :].rearrange("p (e m) -> p e m", e=PAIR),
+                        ALU.mult, ALU.subtract,
+                    )
+                    nc.gpsimd.tensor_scalar(
+                        clipped[u][:, t, :], diff[:, t, :], hi[:, t : t + 1], lo[:, t : t + 1], ALU.min, ALU.max
+                    )
+
+        def gradient(u, copies):
+            o, f = u
+            h_in = sb("h_in%d%d" % u, [P, UNIT, PACK], BF16)
+            h_codes = sb("h_codes%d%d" % u, [P, UNIT], U32)
+            h_scales = sb("h_scales%d%d" % u, [P, UNIT], U8)
+            weights = wt_bank[o][:, PAIR * f : PAIR * (f + 1), :].rearrange("p e (a i) -> p (e a) i", i=4)
+            nc.vector.tensor_tensor(
+                h_in[:].rearrange("p (a i) t -> p a t i", i=4),
+                clipped[u][:].rearrange("p t (a i) -> p a t i", i=4),
+                weights.unsqueeze(2).to_broadcast([P, UNIT // 4, PACK, 4]),
+                ALU.mult,
+            )
+            nc.vector.quantize_mx(h_codes[:].bitcast(E5M2), h_scales[:], h_in[:].rearrange("p c t -> p (c t)"))
+            for e in range(PAIR):
+                bank = psum.tile([P, D], F32, tag="acc", name="g_bank")
+                cols = slice(e * P, (e + 1) * P)
+                nc.tensor.matmul_mx(
+                    bank[:], h_codes[:, cols].bitcast(E5M2), h_scales[:, cols],
+                    ws_codes[:].bitcast(E4M3), ws_scales[:], start=True, stop=True,
+                )
+                copies[e](out_sb[o][:, PAIR * f + e, :], bank[:])
+            rows = slice(PAIR * f, PAIR * (f + 1))
+            nc.sync.dma_start(out_view[o][:, rows, :], out_sb[o][:, rows, :])
+
+        def planes(o, cut):
+            o_in = sb("o_in%d" % o, [P, D, PACK], BF16)
+            o_codes = sb("o_codes%d" % o, [P, D], U32)
+            o_scales = sb("o_scales%d" % o, [P, D], U8)
+            for copy, cols in ((nc.vector.tensor_copy, slice(0, cut)), (nc.scalar.copy, slice(cut, D))):
+                if cols.stop > cols.start:
+                    copy(
+                        o_in[:, cols, :].rearrange("p (c i) t -> p c t i", i=4),
+                        out_sb[o][:, :, cols].rearrange("p t (c i) -> p c t i", i=4),
+                    )
+            nc.vector.quantize_mx(o_codes[:].bitcast(E4M3), o_scales[:], o_in[:].rearrange("p d t -> p (d t)"))
+            nc.sync.dma_start(out_1[o].rearrange("p d l -> p (d l)").bitcast(I32), o_codes[:].bitcast(I32))
+            for q in range(4):
+                (nc.sync if q < 2 or o == 0 else nc.scalar).dma_start(
+                    out_2[o, 4 * q : 4 * q + 4, :].bitcast(I32), o_scales[32 * q : 32 * q + 4, :].bitcast(I32)
+                )
+
+        listed = sb("listed", [P, PACK, SLOTS], BF16)
+        wd_in = sb("wd_in", [P, PACK, P, PACK], BF16)
+        wd_codes = sb("wd_codes", [P, SLOTS], U32)
+        wd_scales = sb("wd_scales", [P, SLOTS], U8)
+        ws_in = sb("ws_in", [P, D, PACK], BF16)
+        ws_codes = sb("ws_codes", [P, D], U32)
+        ws_scales = sb("ws_scales", [P, D], U8)
+        ws_words = ws_in[:].rearrange("q d s -> q (d s)").bitcast(F32).rearrange("q (p b k) -> q p b k", b=2, k=4)
+
+        def turn_w(b):
+            bank = psum.tile([P, 4, P], F32, tag="acc", name="w_bank%d" % b)
+            for k in range(4):
+                words = listed[:, 2 * b + k // 2, :].bitcast(F32)
+                nc.tensor.transpose(bank[:, k, :], words[:, k % 2 :: 2], ident[:])
+            nc.scalar.copy(ws_words[:, :, b, :], bank[:].rearrange("q k p -> q p k"))
+
+        nc.vector.tensor_copy(listed[:, 0, :], table[0][:].indirect(offsets[:]))
+        prepare_x(units[0], nc.vector.tensor_copy)
+        prepare_x(units[1], nc.scalar.copy)
+        for t in range(1, PACK - 1):
+            nc.vector.tensor_copy(listed[:, t, :], table[t][:].indirect(offsets[:]))
+        turn_w(0)
+        cut = 288
+        nc.vector.tensor_copy(listed[:, PACK - 1, :cut], table[PACK - 1][:].indirect(offsets[:, : cut // 16]))
+        nc.scalar.activation(listed[:, PACK - 1, cut:], table[PACK - 1][:].indirect(offsets[:, cut // 16 :]), COPY)
+        for s in (slice(0, 2), slice(2, 4)):
+            nc.vector.tensor_copy(
+                wd_in[:, s].rearrange("p s (a b) t -> p a s b t", b=2),
+                listed[:].rearrange("p t (a b s) -> p a s b t", b=2, s=PACK)[:, :, s],
+            )
+        for s in range(2):
+            cols = slice(s * UNIT, (s + 1) * UNIT)
+            nc.vector.quantize_mx(
+                wd_codes[:, cols].bitcast(E4M3), wd_scales[:, cols],
+                wd_in[:, 2 * s : 2 * s + 2].rearrange("p s m t -> p (s m t)"),
+            )
+        turn_w(1)
+        turn_y(units[0])
+        scores(units[0])
+        nc.vector.quantize_mx(ws_codes[:].bitcast(E4M3), ws_scales[:], ws_in[:].rearrange("q d s -> q (d s)"))
+        for n, u in enumerate(units):
+            last = n + 1 == len(units)
+            if not last:
+                if n + 1 >= 2:
+                    prepare_x(units[n + 1], nc.scalar.copy)
+                turn_y(units[n + 1])
+                scores(units[n + 1])
+            gradient(u, (nc.scalar.copy, nc.vector.tensor_copy if last else nc.scalar.copy))
+            if u[1] == PACK // PAIR - 1:
+                planes(u[0], 336 if last else 0)

@@ -16,214 +16,236 @@ COPY = mybir.ActivationFunctionType.Copy
 
 P = 128
 PACK = 4
-SLOTS, ITEMS, D, R = 512, 2048, 512, 1024
 PASS = P * PACK
+SLOTS, ITEMS, D, R = 512, 2048, 512, 1024
 GROUPS = R // PASS
 PAIR = 2
 UNIT = PAIR * P
+RUN = 4
+LIST_ROWS = 16
+GATHER_CUT = 288
+ROUND_CUT = 336
 FLOPS = 2 * 2 * R * SLOTS * D
 
 
 def tile_attend_ghub_pl_x_ts_kernel(tc, xT, wT, y, wt, ts, offs, out_0, out_1, out_2):
     nc = tc.nc
     units = [(o, f) for o in range(GROUPS) for f in range(PACK // PAIR)]
+    vector_copy, scalar_copy = nc.vector.tensor_copy, nc.scalar.copy
 
     with ExitStack() as ctx:
         held = ctx.enter_context(tc.tile_pool(name="held", bufs=1))
-        psum = ctx.enter_context(tc.psum_pool(name="psum", bufs=2))
+        psum = ctx.enter_context(tc.psum_pool(name="psum", bufs=1))
 
         def sb(name, shape, dtype):
             return held.tile(shape, dtype, name=name, align_bytes=64)
 
-        offsets = held.tile([P, SLOTS // 16], U16, name="offsets")
+        banks = [psum.tile([P, PASS], F32, name="bank%d" % n) for n in range(8)]
+        wt_pair, pair_a, pair_b, pair_c = banks[0:2], banks[2:4], banks[4:6], banks[6:8]
+
+        offsets = held.tile([P, SLOTS // LIST_ROWS], U16, name="offsets")
         table = [sb("table%d" % t, [P, ITEMS], F32) for t in range(PACK)]
         ts_row = sb("ts_row", [P, ITEMS], F32)
         wt_col = sb("wt_col", [P, GROUPS, PACK], F32)
         x_raw = [sb("x_raw%d" % o, [P, PACK, PASS], F32) for o in range(GROUPS)]
         y_raw = {u: sb("y_raw%d%d" % u, [P, PAIR, SLOTS], F32) for u in units}
-
         w_planes = wT.rearrange("(p t) n -> t p n", t=PACK)
         x_view = xT[0].rearrange("(p j) r -> p j r", j=PACK)
-        y_view = y[0].rearrange("(o p t) i -> o p t i", p=P, t=PACK)
-        out_view = out_0[0].rearrange("(o p t) d -> o p t d", p=P, t=PACK)
+        y_view = y[0].rearrange("(o m t) i -> o m t i", m=P, t=PACK)
+        out_view = out_0[0].rearrange("(o m t) d -> o m t d", m=P, t=PACK)
+
+        def load_x(o):
+            nc.sync.dma_start(x_raw[o][:], x_view[:, :, o * PASS : (o + 1) * PASS])
+
+        def load_y(u):
+            o, f = u
+            nc.sync.dma_start(y_raw[u][:], y_view[o][:, PAIR * f : PAIR * (f + 1), :])
 
         nc.sync.dma_start(table[0][:], w_planes[0])
         nc.vector.memset(ts_row[:], 0.0)
         nc.sync.dma_start(ts_row[0:1, :], ts[0:1, :])
         nc.sync.dma_start(offsets[:], offs)
-        nc.scalar.dma_start(wt_col[:], wt[0].rearrange("(o p t) one -> p o (t one)", p=P, t=PACK))
-        nc.sync.dma_start(x_raw[0][:], x_view[:, :, :PASS])
+        nc.scalar.dma_start(wt_col[:], wt[0].rearrange("(o m t) one -> m o (t one)", m=P, t=PACK))
+        load_x(0)
+        for u in units[:2]:
+            load_y(u)
         for t in range(1, PACK):
             nc.sync.dma_start(table[t][:], w_planes[t])
-        for o in range(GROUPS):
-            if o > 0:
-                nc.sync.dma_start(x_raw[o][:], x_view[:, :, o * PASS : (o + 1) * PASS])
-            for f in range(PACK // PAIR):
-                nc.sync.dma_start(y_raw[o, f][:], y_view[o][:, PAIR * f : PAIR * (f + 1), :])
+        load_x(1)
+        for u in units[2:]:
+            load_y(u)
 
         ident = sb("ident", [P, P], F32)
         make_identity(nc, ident[:])
 
-        ts_listed = sb("ts_listed", [P, SLOTS], F32)
-        nc.scalar.activation(ts_listed[:], ts_row[:].indirect(offsets[:]), COPY)
-        ts_bank = psum.tile([P, PACK, P], F32, tag="acc", name="ts_bank")
-        for t in range(PACK):
-            nc.tensor.transpose(ts_bank[:, t, :], ts_listed[:, t::PACK], ident[:])
-        ts_col = sb("ts_col", [P, PACK], F32)
-        ts_sq = sb("ts_sq", [P, PACK], F32)
-        ts_neg = sb("ts_neg", [P, PACK], F32)
-        hi = sb("hi", [P, PACK], F32)
-        lo = sb("lo", [P, PACK], F32)
-        nc.vector.tensor_copy(ts_col[:], ts_bank[:, :, 0])
-        nc.vector.tensor_tensor(ts_sq[:], ts_col[:], ts_col[:], ALU.mult)
-        nc.vector.tensor_scalar(ts_neg[:], ts_col[:], -1.0, None, ALU.mult)
-        nc.vector.tensor_tensor(hi[:], ts_col[:], ts_neg[:], ALU.max)
-        nc.vector.tensor_tensor(lo[:], ts_col[:], ts_neg[:], ALU.min)
-
-        wt_bank = []
         for o in range(GROUPS):
-            bank = psum.tile([P, PACK, P], F32, tag="wt", name="wt_bank%d" % o)
             for t in range(PACK):
-                nc.tensor.transpose(bank[:, t, :], wt_col[:, o, t : t + 1].to_broadcast([P, P]), ident[:])
-            wt_bank.append(bank)
+                column = wt_col[:, o, t : t + 1].to_broadcast([P, P])
+                nc.tensor.transpose(wt_pair[o][:, t * P : (t + 1) * P], column, ident[:])
 
-        x_codes, x_scales, y_scaled, clipped = {}, {}, {}, {}
-        out_sb = [sb("out_sb%d" % o, [P, PACK, D], F32) for o in range(GROUPS)]
+        ts_listed = sb("ts_listed", [P, SLOTS], F32)
+        ts_col, ts_square, ts_minus, upper, lower = [
+            sb(name, [P, PACK], F32) for name in ("ts_col", "ts_square", "ts_minus", "upper", "lower")
+        ]
+        vector_copy(ts_listed[:], ts_row[:].indirect(offsets[:]))
+        for t in range(PACK):
+            nc.tensor.transpose(pair_c[1][:, t * P : (t + 1) * P], ts_listed[:, t::PACK], ident[:])
+        scalar_copy(ts_col[:], pair_c[1][:, ::P])
+        nc.vector.tensor_tensor(ts_square[:], ts_col[:], ts_col[:], ALU.mult)
+        nc.vector.tensor_scalar(ts_minus[:], ts_col[:], -1.0, None, ALU.mult)
+        nc.vector.tensor_tensor(upper[:], ts_col[:], ts_minus[:], ALU.max)
+        nc.vector.tensor_tensor(lower[:], ts_col[:], ts_minus[:], ALU.min)
 
-        def prepare_x(u, copy):
+        listed = sb("listed", [P, PACK, SLOTS], BF16)
+        stage = [sb("stage%d" % n, [P, UNIT, PACK], BF16) for n in range(2)]
+        wd_codes, wd_scales = sb("wd_codes", [P, SLOTS], U32), sb("wd_scales", [P, SLOTS], U8)
+        ws_in = sb("ws_in", [P, D, PACK], BF16)
+        ws_codes, ws_scales = sb("ws_codes", [P, D], U32), sb("ws_scales", [P, D], U8)
+        x_codes = {u: sb("x_codes%d%d" % u, [P, UNIT], U32) for u in units}
+        x_scales = {u: sb("x_scales%d%d" % u, [P, UNIT], U8) for u in units}
+        y_scaled = {u: sb("y_scaled%d%d" % u, [P, PACK, UNIT], F32) for u in units}
+        clipped = {u: sb("clipped%d%d" % u, [P, PACK, UNIT], F32) for u in units}
+        result = [sb("result%d" % o, [P, PACK, D], F32) for o in range(GROUPS)]
+
+        def quantise(codes, scales, values, fmt):
+            nc.vector.quantize_mx(codes.bitcast(fmt), scales, values.rearrange("p c t -> p (c t)"))
+
+        def gather(t, first, last, engine_copy):
+            window = table[t][:].indirect(offsets[:, first // LIST_ROWS : last // LIST_ROWS])
+            engine_copy(listed[:, t, first:last], window)
+
+        def scalar_gather(out, window):
+            nc.scalar.activation(out, window, COPY)
+
+        def deal_w(n, engine_copy):
+            engine_copy(
+                stage[n][:].rearrange("p (s a b) t -> p a s b t", s=2, b=2),
+                listed[:].rearrange("p t (a b s) -> p a s b t", b=2, s=PACK)[:, :, 2 * n : 2 * n + 2],
+            )
+
+        def turn_w(n, bank):
+            for k in range(PACK):
+                words = listed[:, 2 * n + k // 2, :].bitcast(F32)
+                nc.tensor.transpose(bank[:, k * P : (k + 1) * P], words[:, k % 2 :: 2], ident[:])
+            ws_words = ws_in[:].rearrange("q d s -> q (d s)").bitcast(F32)
+            scalar_copy(
+                ws_words.rearrange("q (p n k) -> q p n k", n=2, k=PACK)[:, :, n, :],
+                bank[:].rearrange("q (k p) -> q p k", k=PACK),
+            )
+
+        def prepare_x(u, x_in):
             o, f = u
-            x_in = sb("x_in%d%d" % u, [P, P, PAIR, PACK], BF16)
-            src = x_raw[o][:].rearrange("p j (m f e) -> p f m j e", f=PACK // PAIR, e=PAIR)[:, f]
-            copy(x_in[:].rearrange("p m e j -> p m j e"), src)
-            x_codes[u] = sb("x_codes%d%d" % u, [P, UNIT], U32)
-            x_scales[u] = sb("x_scales%d%d" % u, [P, UNIT], U8)
-            nc.vector.quantize_mx(x_codes[u][:].bitcast(E4M3), x_scales[u][:], x_in[:].rearrange("p m e j -> p (m e j)"))
+            rows = x_raw[o][:].rearrange("p j (m f e) -> p f m j e", f=PACK // PAIR, e=PAIR)[:, f]
+            scalar_copy(x_in[:].rearrange("p (m e) j -> p m j e", e=PAIR), rows)
+            quantise(x_codes[u][:], x_scales[u][:], x_in[:], E4M3)
 
-        def turn_y(u):
-            y_scaled[u] = sb("y_scaled%d%d" % u, [P, PACK, UNIT], F32)
-            for b in range(2):
-                bank = psum.tile([P, 2, PAIR, P], F32, tag="yt", name="y_bank")
+        def turn_y(u, pair):
+            for n, bank in enumerate(pair):
                 for k in range(2):
                     for e in range(PAIR):
-                        nc.tensor.transpose(bank[:, k, e, :], y_raw[u][:, e, 2 * b + k :: PACK], ident[:])
+                        cols = slice(k * UNIT + e * P, k * UNIT + (e + 1) * P)
+                        nc.tensor.transpose(bank[:, cols], y_raw[u][:, e, 2 * n + k :: PACK], ident[:])
                 for k in range(2):
-                    t = 2 * b + k
+                    t = 2 * n + k
                     nc.scalar.activation(
-                        y_scaled[u][:, t, :], bank[:, k].rearrange("p e m -> p (e m)"), COPY, scale=ts_col[:, t : t + 1]
+                        y_scaled[u][:, t, :], bank[:, k * UNIT : (k + 1) * UNIT], COPY, scale=ts_col[:, t : t + 1]
                     )
 
-        def scores(u):
+        def scores(u, pair):
             diff = sb("diff%d%d" % u, [P, PACK, UNIT], F32)
-            clipped[u] = sb("clipped%d%d" % u, [P, PACK, UNIT], F32)
-            for b in range(2):
-                bank = psum.tile([P, 2, UNIT], F32, tag="sc", name="s_bank")
+            for n, bank in enumerate(pair):
                 for k in range(2):
-                    cols = slice((2 * b + k) * P, (2 * b + k + 1) * P)
+                    cols = slice((2 * n + k) * P, (2 * n + k + 1) * P)
                     nc.tensor.matmul_mx(
-                        bank[:, k, :], wd_codes[:, cols].bitcast(E4M3), wd_scales[:, cols],
+                        bank[:, k * UNIT : (k + 1) * UNIT], wd_codes[:, cols].bitcast(E4M3), wd_scales[:, cols],
                         x_codes[u][:].bitcast(E4M3), x_scales[u][:], start=True, stop=True,
                     )
                 for k in range(2):
-                    t = 2 * b + k
+                    t = 2 * n + k
                     nc.vector.scalar_tensor_tensor(
                         diff[:, t, :].rearrange("p (e m) -> p e m", e=PAIR),
-                        bank[:, k, :].rearrange("p (m e) -> p e m", e=PAIR),
-                        ts_sq[:, t : t + 1],
+                        bank[:, k * UNIT : (k + 1) * UNIT].rearrange("p (m e) -> p e m", e=PAIR),
+                        ts_square[:, t : t + 1],
                         y_scaled[u][:, t, :].rearrange("p (e m) -> p e m", e=PAIR),
                         ALU.mult, ALU.subtract,
                     )
-                    nc.gpsimd.tensor_scalar(
-                        clipped[u][:, t, :], diff[:, t, :], hi[:, t : t + 1], lo[:, t : t + 1], ALU.min, ALU.max
-                    )
+            for t in range(PACK):
+                nc.vector.tensor_scalar(
+                    clipped[u][:, t, :], diff[:, t, :], upper[:, t : t + 1], lower[:, t : t + 1], ALU.min, ALU.max
+                )
 
-        def gradient(u, copies):
+        def gradient(u, pair, pieces, copies):
             o, f = u
             h_in = sb("h_in%d%d" % u, [P, UNIT, PACK], BF16)
-            h_codes = sb("h_codes%d%d" % u, [P, UNIT], U32)
-            h_scales = sb("h_scales%d%d" % u, [P, UNIT], U8)
-            weights = wt_bank[o][:, PAIR * f : PAIR * (f + 1), :].rearrange("p e (a i) -> p (e a) i", i=4)
-            nc.vector.tensor_tensor(
-                h_in[:].rearrange("p (a i) t -> p a t i", i=4),
-                clipped[u][:].rearrange("p t (a i) -> p a t i", i=4),
-                weights.unsqueeze(2).to_broadcast([P, UNIT // 4, PACK, 4]),
-                ALU.mult,
-            )
-            nc.vector.quantize_mx(h_codes[:].bitcast(E5M2), h_scales[:], h_in[:].rearrange("p c t -> p (c t)"))
+            h_codes, h_scales = sb("h_codes%d%d" % u, [P, UNIT], U32), sb("h_scales%d%d" % u, [P, UNIT], U8)
+            width = UNIT // pieces
+            parts = [slice(n * width, (n + 1) * width) for n in range(pieces)]
+            for cols in parts:
+                weights = wt_pair[o][:, f * UNIT : (f + 1) * UNIT][:, cols].rearrange("p (a i) -> p a i", i=RUN)
+                nc.vector.tensor_tensor(
+                    h_in[:, cols].rearrange("p (a i) t -> p a t i", i=RUN),
+                    clipped[u][:, :, cols].rearrange("p t (a i) -> p a t i", i=RUN),
+                    weights.unsqueeze(2).to_broadcast([P, width // RUN, PACK, RUN]),
+                    ALU.mult,
+                )
+            for cols in parts:
+                quantise(h_codes[:, cols], h_scales[:, cols], h_in[:, cols], E5M2)
             for e in range(PAIR):
-                bank = psum.tile([P, D], F32, tag="acc", name="g_bank")
                 cols = slice(e * P, (e + 1) * P)
                 nc.tensor.matmul_mx(
-                    bank[:], h_codes[:, cols].bitcast(E5M2), h_scales[:, cols],
+                    pair[e][:], h_codes[:, cols].bitcast(E5M2), h_scales[:, cols],
                     ws_codes[:].bitcast(E4M3), ws_scales[:], start=True, stop=True,
                 )
-                copies[e](out_sb[o][:, PAIR * f + e, :], bank[:])
+                copies[e](result[o][:, PAIR * f + e, :], pair[e][:])
             rows = slice(PAIR * f, PAIR * (f + 1))
-            nc.sync.dma_start(out_view[o][:, rows, :], out_sb[o][:, rows, :])
+            nc.sync.dma_start(out_view[o][:, rows, :], result[o][:, rows, :])
 
-        def planes(o, cut):
+        def planes(o, shares, scale_queues):
             o_in = sb("o_in%d" % o, [P, D, PACK], BF16)
-            o_codes = sb("o_codes%d" % o, [P, D], U32)
-            o_scales = sb("o_scales%d" % o, [P, D], U8)
-            for copy, cols in ((nc.vector.tensor_copy, slice(0, cut)), (nc.scalar.copy, slice(cut, D))):
-                if cols.stop > cols.start:
-                    copy(
-                        o_in[:, cols, :].rearrange("p (c i) t -> p c t i", i=4),
-                        out_sb[o][:, :, cols].rearrange("p t (c i) -> p c t i", i=4),
-                    )
-            nc.vector.quantize_mx(o_codes[:].bitcast(E4M3), o_scales[:], o_in[:].rearrange("p d t -> p (d t)"))
+            o_codes, o_scales = sb("o_codes%d" % o, [P, D], U32), sb("o_scales%d" % o, [P, D], U8)
+            for engine_copy, cols in shares:
+                engine_copy(
+                    o_in[:, cols, :].rearrange("p (c i) t -> p c t i", i=RUN),
+                    result[o][:, :, cols].rearrange("p t (c i) -> p c t i", i=RUN),
+                )
+            quantise(o_codes[:], o_scales[:], o_in[:], E4M3)
             nc.sync.dma_start(out_1[o].rearrange("p d l -> p (d l)").bitcast(I32), o_codes[:].bitcast(I32))
-            for q in range(4):
-                (nc.sync if q < 2 or o == 0 else nc.scalar).dma_start(
+            for q, queue in enumerate(scale_queues):
+                queue.dma_start(
                     out_2[o, 4 * q : 4 * q + 4, :].bitcast(I32), o_scales[32 * q : 32 * q + 4, :].bitcast(I32)
                 )
 
-        listed = sb("listed", [P, PACK, SLOTS], BF16)
-        wd_in = sb("wd_in", [P, PACK, P, PACK], BF16)
-        wd_codes = sb("wd_codes", [P, SLOTS], U32)
-        wd_scales = sb("wd_scales", [P, SLOTS], U8)
-        ws_in = sb("ws_in", [P, D, PACK], BF16)
-        ws_codes = sb("ws_codes", [P, D], U32)
-        ws_scales = sb("ws_scales", [P, D], U8)
-        ws_words = ws_in[:].rearrange("q d s -> q (d s)").bitcast(F32).rearrange("q (p b k) -> q p b k", b=2, k=4)
+        gather(0, 0, SLOTS, vector_copy)
+        for n in range(2):
+            prepare_x(units[n], sb("x_in%d" % n, [P, UNIT, PACK], BF16))
+        turn_y(units[0], pair_a)
+        turn_y(units[1], pair_b)
+        gather(1, 0, SLOTS, vector_copy)
+        gather(2, 0, SLOTS, vector_copy)
+        turn_w(0, pair_c[0])
 
-        def turn_w(b):
-            bank = psum.tile([P, 4, P], F32, tag="acc", name="w_bank%d" % b)
-            for k in range(4):
-                words = listed[:, 2 * b + k // 2, :].bitcast(F32)
-                nc.tensor.transpose(bank[:, k, :], words[:, k % 2 :: 2], ident[:])
-            nc.scalar.copy(ws_words[:, :, b, :], bank[:].rearrange("q k p -> q p k"))
+        gather(3, 0, GATHER_CUT, vector_copy)
+        gather(3, GATHER_CUT, SLOTS, scalar_gather)
+        deal_w(0, vector_copy)
+        deal_w(1, scalar_copy)
+        for n in range(2):
+            cols = slice(n * UNIT, (n + 1) * UNIT)
+            quantise(wd_codes[:, cols], wd_scales[:, cols], stage[n][:], E4M3)
 
-        nc.vector.tensor_copy(listed[:, 0, :], table[0][:].indirect(offsets[:]))
-        prepare_x(units[0], nc.vector.tensor_copy)
-        prepare_x(units[1], nc.scalar.copy)
-        for t in range(1, PACK - 1):
-            nc.vector.tensor_copy(listed[:, t, :], table[t][:].indirect(offsets[:]))
-        turn_w(0)
-        cut = 288
-        nc.vector.tensor_copy(listed[:, PACK - 1, :cut], table[PACK - 1][:].indirect(offsets[:, : cut // 16]))
-        nc.scalar.activation(listed[:, PACK - 1, cut:], table[PACK - 1][:].indirect(offsets[:, cut // 16 :]), COPY)
-        for s in (slice(0, 2), slice(2, 4)):
-            nc.vector.tensor_copy(
-                wd_in[:, s].rearrange("p s (a b) t -> p a s b t", b=2),
-                listed[:].rearrange("p t (a b s) -> p a s b t", b=2, s=PACK)[:, :, s],
-            )
-        for s in range(2):
-            cols = slice(s * UNIT, (s + 1) * UNIT)
-            nc.vector.quantize_mx(
-                wd_codes[:, cols].bitcast(E4M3), wd_scales[:, cols],
-                wd_in[:, 2 * s : 2 * s + 2].rearrange("p s m t -> p (s m t)"),
-            )
-        turn_w(1)
-        turn_y(units[0])
-        scores(units[0])
-        nc.vector.quantize_mx(ws_codes[:].bitcast(E4M3), ws_scales[:], ws_in[:].rearrange("q d s -> q (d s)"))
-        for n, u in enumerate(units):
-            last = n + 1 == len(units)
-            if not last:
-                if n + 1 >= 2:
-                    prepare_x(units[n + 1], nc.scalar.copy)
-                turn_y(units[n + 1])
-                scores(units[n + 1])
-            gradient(u, (nc.scalar.copy, nc.vector.tensor_copy if last else nc.scalar.copy))
-            if u[1] == PACK // PAIR - 1:
-                planes(u[0], 336 if last else 0)
+        scores(units[0], pair_a)
+        turn_w(1, pair_c[1])
+        quantise(ws_codes[:], ws_scales[:], ws_in[:], E4M3)
+        scores(units[1], pair_b)
+        prepare_x(units[2], stage[0])
+        turn_y(units[2], pair_a)
+        gradient(units[0], pair_c, 1, (scalar_copy, scalar_copy))
+        scores(units[2], pair_b)
+        prepare_x(units[3], stage[1])
+        turn_y(units[3], pair_a)
+        gradient(units[1], pair_c, 1, (scalar_copy, scalar_copy))
+        scores(units[3], pair_b)
+        planes(0, [(scalar_copy, slice(0, D))], [nc.sync] * 4)
+        gradient(units[2], pair_c, 1, (scalar_copy, scalar_copy))
+        gradient(units[3], pair_a, PAIR, (scalar_copy, vector_copy))
+        shares = [(vector_copy, slice(0, ROUND_CUT)), (scalar_copy, slice(ROUND_CUT, D))]
+        planes(1, shares, [nc.sync, nc.sync, nc.scalar, nc.scalar])

@@ -19,9 +19,7 @@ PACK = 4
 PASS = P * PACK
 SLOTS, ITEMS, D, R = 512, 2048, 512, 1024
 GROUPS = R // PASS
-PAIR = 2
-UNIT = PAIR * P
-RUN = 4
+LINE = 4
 LIST_ROWS = 16
 GATHER_CUT = 288
 ROUND_CUT = 336
@@ -30,7 +28,6 @@ FLOPS = 2 * 2 * R * SLOTS * D
 
 def tile_attend_ghub_pl_x_ts_kernel(tc, xT, wT, y, wt, ts, offs, out_0, out_1, out_2):
     nc = tc.nc
-    units = [(o, f) for o in range(GROUPS) for f in range(PACK // PAIR)]
     vector_copy, scalar_copy = nc.vector.tensor_copy, nc.scalar.copy
 
     with ExitStack() as ctx:
@@ -41,47 +38,40 @@ def tile_attend_ghub_pl_x_ts_kernel(tc, xT, wT, y, wt, ts, offs, out_0, out_1, o
             return held.tile(shape, dtype, name=name, align_bytes=64)
 
         banks = [psum.tile([P, PASS], F32, name="bank%d" % n) for n in range(8)]
-        wt_pair, pair_a, pair_b, pair_c = banks[0:2], banks[2:4], banks[4:6], banks[6:8]
+        wt_banks, quad, spare = banks[0:2], banks[2:6], banks[6:8]
 
         offsets = held.tile([P, SLOTS // LIST_ROWS], U16, name="offsets")
         table = [sb("table%d" % t, [P, ITEMS], F32) for t in range(PACK)]
         ts_row = sb("ts_row", [P, ITEMS], F32)
         wt_col = sb("wt_col", [P, GROUPS, PACK], F32)
         x_raw = [sb("x_raw%d" % o, [P, PACK, PASS], F32) for o in range(GROUPS)]
-        y_raw = {u: sb("y_raw%d%d" % u, [P, PAIR, SLOTS], F32) for u in units}
+        y_raw = [sb("y_raw%d" % o, [P, PACK, SLOTS], F32) for o in range(GROUPS)]
         w_planes = wT.rearrange("(p t) n -> t p n", t=PACK)
         x_view = xT[0].rearrange("(p j) r -> p j r", j=PACK)
-        y_view = y[0].rearrange("(o m t) i -> o m t i", m=P, t=PACK)
-        out_view = out_0[0].rearrange("(o m t) d -> o m t d", m=P, t=PACK)
+        y_view = y[0].rearrange("(o m e) i -> o m e i", m=P, e=PACK)
+        out_view = out_0[0].rearrange("(o m e) d -> o m e d", m=P, e=PACK)
 
-        def load_x(o):
+        def load_rows(o):
             nc.sync.dma_start(x_raw[o][:], x_view[:, :, o * PASS : (o + 1) * PASS])
-
-        def load_y(u):
-            o, f = u
-            nc.sync.dma_start(y_raw[u][:], y_view[o][:, PAIR * f : PAIR * (f + 1), :])
+            nc.sync.dma_start(y_raw[o][:], y_view[o])
 
         nc.sync.dma_start(table[0][:], w_planes[0])
         nc.vector.memset(ts_row[:], 0.0)
         nc.sync.dma_start(ts_row[0:1, :], ts[0:1, :])
         nc.sync.dma_start(offsets[:], offs)
-        nc.scalar.dma_start(wt_col[:], wt[0].rearrange("(o m t) one -> m o (t one)", m=P, t=PACK))
-        load_x(0)
-        for u in units[:2]:
-            load_y(u)
+        nc.scalar.dma_start(wt_col[:], wt[0].rearrange("(o m e) one -> m o (e one)", m=P, e=PACK))
+        load_rows(0)
         for t in range(1, PACK):
             nc.sync.dma_start(table[t][:], w_planes[t])
-        load_x(1)
-        for u in units[2:]:
-            load_y(u)
+        load_rows(1)
 
         ident = sb("ident", [P, P], F32)
         make_identity(nc, ident[:])
 
         for o in range(GROUPS):
-            for t in range(PACK):
-                column = wt_col[:, o, t : t + 1].to_broadcast([P, P])
-                nc.tensor.transpose(wt_pair[o][:, t * P : (t + 1) * P], column, ident[:])
+            for e in range(PACK):
+                column = wt_col[:, o, e : e + 1].to_broadcast([P, P])
+                nc.tensor.transpose(wt_banks[o][:, e * P : (e + 1) * P], column, ident[:])
 
         ts_listed = sb("ts_listed", [P, SLOTS], F32)
         ts_col, ts_square, ts_minus, upper, lower = [
@@ -89,23 +79,23 @@ def tile_attend_ghub_pl_x_ts_kernel(tc, xT, wT, y, wt, ts, offs, out_0, out_1, o
         ]
         vector_copy(ts_listed[:], ts_row[:].indirect(offsets[:]))
         for t in range(PACK):
-            nc.tensor.transpose(pair_c[1][:, t * P : (t + 1) * P], ts_listed[:, t::PACK], ident[:])
-        scalar_copy(ts_col[:], pair_c[1][:, ::P])
+            nc.tensor.transpose(spare[1][:, t * P : (t + 1) * P], ts_listed[:, t::PACK], ident[:])
+        scalar_copy(ts_col[:], spare[1][:, ::P])
         nc.vector.tensor_tensor(ts_square[:], ts_col[:], ts_col[:], ALU.mult)
         nc.vector.tensor_scalar(ts_minus[:], ts_col[:], -1.0, None, ALU.mult)
         nc.vector.tensor_tensor(upper[:], ts_col[:], ts_minus[:], ALU.max)
         nc.vector.tensor_tensor(lower[:], ts_col[:], ts_minus[:], ALU.min)
 
         listed = sb("listed", [P, PACK, SLOTS], BF16)
-        stage = [sb("stage%d" % n, [P, UNIT, PACK], BF16) for n in range(2)]
+        stage = sb("stage", [P, PASS, PACK], BF16)
         wd_codes, wd_scales = sb("wd_codes", [P, SLOTS], U32), sb("wd_scales", [P, SLOTS], U8)
-        ws_in = sb("ws_in", [P, D, PACK], BF16)
         ws_codes, ws_scales = sb("ws_codes", [P, D], U32), sb("ws_scales", [P, D], U8)
-        x_codes = {u: sb("x_codes%d%d" % u, [P, UNIT], U32) for u in units}
-        x_scales = {u: sb("x_scales%d%d" % u, [P, UNIT], U8) for u in units}
-        y_scaled = {u: sb("y_scaled%d%d" % u, [P, PACK, UNIT], F32) for u in units}
-        clipped = {u: sb("clipped%d%d" % u, [P, PACK, UNIT], F32) for u in units}
+        x_codes = [sb("x_codes%d" % o, [P, PASS], U32) for o in range(GROUPS)]
+        x_scales = [sb("x_scales%d" % o, [P, PASS], U8) for o in range(GROUPS)]
+        y_scaled = [sb("y_scaled%d" % o, [P, PACK, PASS], F32) for o in range(GROUPS)]
+        clipped = [sb("clipped%d" % o, [P, PACK, PASS], F32) for o in range(GROUPS)]
         result = [sb("result%d" % o, [P, PACK, D], F32) for o in range(GROUPS)]
+        halves = [slice(0, PASS // 2), slice(PASS // 2, PASS)]
 
         def quantise(codes, scales, values, fmt):
             nc.vector.quantize_mx(codes.bitcast(fmt), scales, values.rearrange("p c t -> p (c t)"))
@@ -117,135 +107,134 @@ def tile_attend_ghub_pl_x_ts_kernel(tc, xT, wT, y, wt, ts, offs, out_0, out_1, o
         def scalar_gather(out, window):
             nc.scalar.activation(out, window, COPY)
 
+        def interleave(engine_copy, out, planes):
+            engine_copy(out.rearrange("p (c i) t -> p c t i", i=LINE), planes.rearrange("p t (c i) -> p c t i", i=LINE))
+
         def deal_w(n, engine_copy):
             engine_copy(
-                stage[n][:].rearrange("p (s a b) t -> p a s b t", s=2, b=2),
+                stage[:, halves[n]].rearrange("p (s a b) t -> p a s b t", s=2, b=2),
                 listed[:].rearrange("p t (a b s) -> p a s b t", b=2, s=PACK)[:, :, 2 * n : 2 * n + 2],
             )
 
-        def turn_w(n, bank):
-            for k in range(PACK):
-                words = listed[:, 2 * n + k // 2, :].bitcast(F32)
-                nc.tensor.transpose(bank[:, k * P : (k + 1) * P], words[:, k % 2 :: 2], ident[:])
-            ws_words = ws_in[:].rearrange("q d s -> q (d s)").bitcast(F32)
+        def turn_w(n):
+            ws_in = sb("ws_in%d" % n, [P, D // 2, PACK], BF16)
+            for k in range(2):
+                words = listed[:, 2 * n + k, :].bitcast(F32)
+                for u in range(2):
+                    cols = slice((2 * k + u) * P, (2 * k + u + 1) * P)
+                    nc.tensor.transpose(spare[n][:, cols], words[:, u::2], ident[:])
             scalar_copy(
-                ws_words.rearrange("q (p n k) -> q p n k", n=2, k=PACK)[:, :, n, :],
-                bank[:].rearrange("q (k p) -> q p k", k=PACK),
+                ws_in[:].rearrange("q d s -> q (d s)").bitcast(F32).rearrange("q (p ku) -> q p ku", ku=PACK),
+                spare[n][:].rearrange("q (ku p) -> q p ku", ku=PACK),
             )
+            quantise(ws_codes[:, halves[n]], ws_scales[:, halves[n]], ws_in[:], E4M3)
 
-        def prepare_x(u, x_in):
-            o, f = u
-            rows = x_raw[o][:].rearrange("p j (m f e) -> p f m j e", f=PACK // PAIR, e=PAIR)[:, f]
-            scalar_copy(x_in[:].rearrange("p (m e) j -> p m j e", e=PAIR), rows)
-            quantise(x_codes[u][:], x_scales[u][:], x_in[:], E4M3)
+        def prepare_x(o, x_in):
+            for cols in halves:
+                interleave(scalar_copy, x_in[:, cols], x_raw[o][:, :, cols])
+            quantise(x_codes[o][:], x_scales[o][:], x_in[:], E4M3)
 
-        def turn_y(u, pair):
-            for n, bank in enumerate(pair):
-                for k in range(2):
-                    for e in range(PAIR):
-                        cols = slice(k * UNIT + e * P, k * UNIT + (e + 1) * P)
-                        nc.tensor.transpose(bank[:, cols], y_raw[u][:, e, 2 * n + k :: PACK], ident[:])
-                for k in range(2):
-                    t = 2 * n + k
-                    nc.scalar.activation(
-                        y_scaled[u][:, t, :], bank[:, k * UNIT : (k + 1) * UNIT], COPY, scale=ts_col[:, t : t + 1]
-                    )
+        def turn_y(o):
+            for t in range(PACK):
+                for e in range(PACK):
+                    nc.tensor.transpose(quad[t][:, e * P : (e + 1) * P], y_raw[o][:, e, t::PACK], ident[:])
+                nc.scalar.activation(y_scaled[o][:, t, :], quad[t][:], COPY, scale=ts_col[:, t : t + 1])
 
-        def scores(u, pair):
-            diff = sb("diff%d%d" % u, [P, PACK, UNIT], F32)
-            for n, bank in enumerate(pair):
-                for k in range(2):
-                    cols = slice((2 * n + k) * P, (2 * n + k + 1) * P)
-                    nc.tensor.matmul_mx(
-                        bank[:, k * UNIT : (k + 1) * UNIT], wd_codes[:, cols].bitcast(E4M3), wd_scales[:, cols],
-                        x_codes[u][:].bitcast(E4M3), x_scales[u][:], start=True, stop=True,
-                    )
-                for k in range(2):
-                    t = 2 * n + k
-                    nc.vector.scalar_tensor_tensor(
-                        diff[:, t, :].rearrange("p (e m) -> p e m", e=PAIR),
-                        bank[:, k * UNIT : (k + 1) * UNIT].rearrange("p (m e) -> p e m", e=PAIR),
-                        ts_square[:, t : t + 1],
-                        y_scaled[u][:, t, :].rearrange("p (e m) -> p e m", e=PAIR),
-                        ALU.mult, ALU.subtract,
-                    )
+        def scores(o):
+            diff = sb("diff%d" % o, [P, PACK, PASS], F32)
+            for t in range(PACK):
+                cols = slice(t * P, (t + 1) * P)
+                nc.tensor.matmul_mx(
+                    quad[t][:], wd_codes[:, cols].bitcast(E4M3), wd_scales[:, cols],
+                    x_codes[o][:].bitcast(E4M3), x_scales[o][:], start=True, stop=True,
+                )
+                nc.vector.scalar_tensor_tensor(
+                    diff[:, t, :].rearrange("p (e m) -> p e m", e=PACK),
+                    quad[t][:].rearrange("p (m e) -> p e m", e=PACK),
+                    ts_square[:, t : t + 1],
+                    y_scaled[o][:, t, :].rearrange("p (e m) -> p e m", e=PACK),
+                    ALU.mult, ALU.subtract,
+                )
             for t in range(PACK):
                 nc.vector.tensor_scalar(
-                    clipped[u][:, t, :], diff[:, t, :], upper[:, t : t + 1], lower[:, t : t + 1], ALU.min, ALU.max
+                    clipped[o][:, t, :], diff[:, t, :], upper[:, t : t + 1], lower[:, t : t + 1], ALU.min, ALU.max
                 )
 
-        def gradient(u, pair, pieces, copies):
-            o, f = u
-            h_in = sb("h_in%d%d" % u, [P, UNIT, PACK], BF16)
-            h_codes, h_scales = sb("h_codes%d%d" % u, [P, UNIT], U32), sb("h_scales%d%d" % u, [P, UNIT], U8)
-            width = UNIT // pieces
+        def gradient(o, pieces, out_banks, copies, tiles_a_store):
+            h_in = sb("h_in%d" % o, [P, PASS, PACK], BF16)
+            h_codes, h_scales = sb("h_codes%d" % o, [P, PASS], U32), sb("h_scales%d" % o, [P, PASS], U8)
+            width = PASS // pieces
             parts = [slice(n * width, (n + 1) * width) for n in range(pieces)]
-            for cols in parts:
-                weights = wt_pair[o][:, f * UNIT : (f + 1) * UNIT][:, cols].rearrange("p (a i) -> p a i", i=RUN)
+
+            def weigh(cols):
+                weights = wt_banks[o][:, cols].rearrange("p (a i) -> p a i", i=2)
                 nc.vector.tensor_tensor(
-                    h_in[:, cols].rearrange("p (a i) t -> p a t i", i=RUN),
-                    clipped[u][:, :, cols].rearrange("p t (a i) -> p a t i", i=RUN),
-                    weights.unsqueeze(2).to_broadcast([P, width // RUN, PACK, RUN]),
+                    h_in[:, cols].rearrange("p (a i) t -> p a t i", i=2),
+                    clipped[o][:, :, cols].rearrange("p t (a i) -> p a t i", i=2),
+                    weights.unsqueeze(2).to_broadcast([P, width // 2, PACK, 2]),
                     ALU.mult,
                 )
-            for cols in parts:
-                quantise(h_codes[:, cols], h_scales[:, cols], h_in[:, cols], E5M2)
-            for e in range(PAIR):
-                cols = slice(e * P, (e + 1) * P)
-                nc.tensor.matmul_mx(
-                    pair[e][:], h_codes[:, cols].bitcast(E5M2), h_scales[:, cols],
-                    ws_codes[:].bitcast(E4M3), ws_scales[:], start=True, stop=True,
-                )
-                copies[e](result[o][:, PAIR * f + e, :], pair[e][:])
-            rows = slice(PAIR * f, PAIR * (f + 1))
-            nc.sync.dma_start(out_view[o][:, rows, :], result[o][:, rows, :])
 
-        def planes(o, shares, scale_queues):
+            def multiply(cols):
+                quantise(h_codes[:, cols], h_scales[:, cols], h_in[:, cols], E5M2)
+                for e in range(cols.start // P, cols.stop // P):
+                    tile = slice(e * P, (e + 1) * P)
+                    nc.tensor.matmul_mx(
+                        out_banks[e][:], h_codes[:, tile].bitcast(E5M2), h_scales[:, tile],
+                        ws_codes[:].bitcast(E4M3), ws_scales[:], start=True, stop=True,
+                    )
+                    copies[e](
+                        result[o][:, e, :].rearrange("m (p n k) -> m p n k", n=2, k=2),
+                        out_banks[e][:].rearrange("m (n p k) -> m p n k", n=2, k=2),
+                    )
+                    if (e + 1) % tiles_a_store == 0:
+                        rows = slice(e + 1 - tiles_a_store, e + 1)
+                        nc.sync.dma_start(out_view[o][:, rows, :], result[o][:, rows, :])
+
+            weigh(parts[0])
+            for done, coming in zip(parts, parts[1:]):
+                weigh(coming)
+                multiply(done)
+            multiply(parts[-1])
+
+        def round_result(o, shares):
             o_in = sb("o_in%d" % o, [P, D, PACK], BF16)
-            o_codes, o_scales = sb("o_codes%d" % o, [P, D], U32), sb("o_scales%d" % o, [P, D], U8)
             for engine_copy, cols in shares:
-                engine_copy(
-                    o_in[:, cols, :].rearrange("p (c i) t -> p c t i", i=RUN),
-                    result[o][:, :, cols].rearrange("p t (c i) -> p c t i", i=RUN),
-                )
-            quantise(o_codes[:], o_scales[:], o_in[:], E4M3)
+                interleave(engine_copy, o_in[:, cols], result[o][:, :, cols])
+            return o_in
+
+        o_scales = sb("o_scales", [P, GROUPS, D], U8)
+
+        def planes(o, o_in):
+            o_codes = sb("o_codes%d" % o, [P, D], U32)
+            quantise(o_codes[:], o_scales[:, o, :], o_in[:], E4M3)
             nc.sync.dma_start(out_1[o].rearrange("p d l -> p (d l)").bitcast(I32), o_codes[:].bitcast(I32))
-            for q, queue in enumerate(scale_queues):
-                queue.dma_start(
-                    out_2[o, 4 * q : 4 * q + 4, :].bitcast(I32), o_scales[32 * q : 32 * q + 4, :].bitcast(I32)
-                )
 
         gather(0, 0, SLOTS, vector_copy)
-        for n in range(2):
-            prepare_x(units[n], sb("x_in%d" % n, [P, UNIT, PACK], BF16))
-        turn_y(units[0], pair_a)
-        turn_y(units[1], pair_b)
+        prepare_x(0, sb("x_first", [P, PASS, PACK], BF16))
+        turn_y(0)
         gather(1, 0, SLOTS, vector_copy)
+        turn_w(0)
         gather(2, 0, SLOTS, vector_copy)
-        turn_w(0, pair_c[0])
 
         gather(3, 0, GATHER_CUT, vector_copy)
         gather(3, GATHER_CUT, SLOTS, scalar_gather)
         deal_w(0, vector_copy)
         deal_w(1, scalar_copy)
-        for n in range(2):
-            cols = slice(n * UNIT, (n + 1) * UNIT)
-            quantise(wd_codes[:, cols], wd_scales[:, cols], stage[n][:], E4M3)
+        for cols in halves:
+            quantise(wd_codes[:, cols], wd_scales[:, cols], stage[:, cols], E4M3)
 
-        scores(units[0], pair_a)
-        turn_w(1, pair_c[1])
-        quantise(ws_codes[:], ws_scales[:], ws_in[:], E4M3)
-        scores(units[1], pair_b)
-        prepare_x(units[2], stage[0])
-        turn_y(units[2], pair_a)
-        gradient(units[0], pair_c, 1, (scalar_copy, scalar_copy))
-        scores(units[2], pair_b)
-        prepare_x(units[3], stage[1])
-        turn_y(units[3], pair_a)
-        gradient(units[1], pair_c, 1, (scalar_copy, scalar_copy))
-        scores(units[3], pair_b)
-        planes(0, [(scalar_copy, slice(0, D))], [nc.sync] * 4)
-        gradient(units[2], pair_c, 1, (scalar_copy, scalar_copy))
-        gradient(units[3], pair_a, PAIR, (scalar_copy, vector_copy))
+        scores(0)
+        turn_w(1)
+        prepare_x(1, stage)
+        turn_y(1)
+        gradient(0, 2, spare + spare, [scalar_copy] * PACK, 2)
+        scores(1)
+        first_rounded = round_result(0, [(scalar_copy, cols) for cols in halves])
+        gradient(1, PACK, quad, [scalar_copy] * (PACK - 1) + [vector_copy], 1)
+        planes(0, first_rounded)
         shares = [(vector_copy, slice(0, ROUND_CUT)), (scalar_copy, slice(ROUND_CUT, D))]
-        planes(1, shares, [nc.sync, nc.sync, nc.scalar, nc.scalar])
+        planes(1, round_result(1, shares))
+        for q, queue in enumerate((nc.scalar, nc.scalar, nc.sync, nc.sync)):
+            scale_rows = out_2[:, 4 * q : 4 * q + 4, :].rearrange("o f d -> f o d")
+            queue.dma_start(scale_rows.bitcast(I32), o_scales[32 * q : 32 * q + 4].bitcast(I32))

@@ -130,8 +130,10 @@ def tile_attend_ghub_pl_x_ts_kernel(tc, xT, wT, y, wt, ts, offs, out_0, out_1, o
             quantise(ws_codes[:, halves[n]], ws_scales[:, halves[n]], ws_in[:], E4M3)
 
         def prepare_x(o, x_in):
-            for cols in halves:
-                interleave(scalar_copy, x_in[:, cols], x_raw[o][:, :, cols])
+            dealt = x_in[:].rearrange("p (e m) j -> p m j e", e=PACK)
+            rows = x_raw[o][:].rearrange("p j (m e) -> p m j e", e=PACK)
+            for ms in (slice(0, P // 2), slice(P // 2, P)):
+                scalar_copy(dealt[:, ms], rows[:, ms])
             quantise(x_codes[o][:], x_scales[o][:], x_in[:], E4M3)
 
         def turn_y(o):
@@ -149,10 +151,7 @@ def tile_attend_ghub_pl_x_ts_kernel(tc, xT, wT, y, wt, ts, offs, out_0, out_1, o
                     x_codes[o][:].bitcast(E4M3), x_scales[o][:], start=True, stop=True,
                 )
                 nc.vector.scalar_tensor_tensor(
-                    diff[:, t, :].rearrange("p (e m) -> p e m", e=PACK),
-                    quad[t][:].rearrange("p (m e) -> p e m", e=PACK),
-                    ts_square[:, t : t + 1],
-                    y_scaled[o][:, t, :].rearrange("p (e m) -> p e m", e=PACK),
+                    diff[:, t, :], quad[t][:], ts_square[:, t : t + 1], y_scaled[o][:, t, :],
                     ALU.mult, ALU.subtract,
                 )
             for t in range(PACK):

@@ -23,6 +23,7 @@ LINE = 4
 LIST_ROWS = 16
 GATHER_CUT = 288
 ROUND_CUT = 336
+GPSIMD_CLIPS = 2
 FLOPS = 2 * 2 * R * SLOTS * D
 
 
@@ -155,7 +156,8 @@ def tile_attend_ghub_pl_x_ts_kernel(tc, xT, wT, y, wt, ts, offs, out_0, out_1, o
                     ALU.mult, ALU.subtract,
                 )
             for t in range(PACK):
-                nc.vector.tensor_scalar(
+                engine = nc.gpsimd if t < GPSIMD_CLIPS else nc.vector
+                engine.tensor_scalar(
                     clipped[o][:, t, :], diff[:, t, :], upper[:, t : t + 1], lower[:, t : t + 1], ALU.min, ALU.max
                 )
 

from contextlib import ExitStack

import concourse.mybir as mybir
from concourse.masks import make_identity

F32 = mybir.dt.float32
BF16 = mybir.dt.bfloat16
I32 = mybir.dt.int32
U32 = mybir.dt.uint32
U16 = mybir.dt.uint16
U8 = mybir.dt.uint8
E4M3 = mybir.dt.float8_e4m3fn_x4
E5M2 = mybir.dt.float8_e5m2_x4
ALU = mybir.AluOpType
COPY = mybir.ActivationFunctionType.Copy

P = 128
PACK = 4
PASS = P * PACK
SLOTS, ITEMS, D, R = 512, 2048, 512, 1024
GROUPS = R // PASS
LINE = 4
LIST_ROWS = 16
GATHER_CUT = 288
ROUND_CUT = 336
GPSIMD_CLIPS = 2
FLOPS = 2 * 2 * R * SLOTS * D


def tile_attend_ghub_pl_x_ts_kernel(tc, xT, wT, y, wt, ts, offs, out_0, out_1, out_2):
    nc = tc.nc
    vector_copy, scalar_copy = nc.vector.tensor_copy, nc.scalar.copy

    with ExitStack() as ctx:
        held = ctx.enter_context(tc.tile_pool(name="held", bufs=1))
        psum = ctx.enter_context(tc.psum_pool(name="psum", bufs=1))

        def sb(name, shape, dtype):
            return held.tile(shape, dtype, name=name, align_bytes=64)

        banks = [psum.tile([P, PASS], F32, name="bank%d" % n) for n in range(8)]
        wt_banks, quad, spare = banks[0:2], banks[2:6], banks[6:8]

        offsets = held.tile([P, SLOTS // LIST_ROWS], U16, name="offsets")
        table = [sb("table%d" % t, [P, ITEMS], F32) for t in range(PACK)]
        ts_row = sb("ts_row", [P, ITEMS], F32)
        wt_col = sb("wt_col", [P, GROUPS, PACK], F32)
        x_raw = [sb("x_raw%d" % o, [P, PACK, PASS], F32) for o in range(GROUPS)]
        y_raw = [sb("y_raw%d" % o, [P, PACK, SLOTS], F32) for o in range(GROUPS)]
        w_planes = wT.rearrange("(p t) n -> t p n", t=PACK)
        x_view = xT[0].rearrange("(p j) r -> p j r", j=PACK)
        y_view = y[0].rearrange("(o m e) i -> o m e i", m=P, e=PACK)
        out_view = out_0[0].rearrange("(o m e) d -> o m e d", m=P, e=PACK)

        def load_rows(o):
            nc.sync.dma_start(x_raw[o][:], x_view[:, :, o * PASS : (o + 1) * PASS])
            nc.sync.dma_start(y_raw[o][:], y_view[o])

        nc.sync.dma_start(table[0][:], w_planes[0])
        nc.vector.memset(ts_row[:], 0.0)
        nc.sync.dma_start(ts_row[0:1, :], ts[0:1, :])
        nc.sync.dma_start(offsets[:], offs)
        nc.scalar.dma_start(wt_col[:], wt[0].rearrange("(o m e) one -> m o (e one)", m=P, e=PACK))
        load_rows(0)
        for t in range(1, PACK):
            nc.sync.dma_start(table[t][:], w_planes[t])
        load_rows(1)

        ident = sb("ident", [P, P], F32)
        make_identity(nc, ident[:])

        for o in range(GROUPS):
            for e in range(PACK):
                column = wt_col[:, o, e : e + 1].to_broadcast([P, P])
                nc.tensor.transpose(wt_banks[o][:, e * P : (e + 1) * P], column, ident[:])

        ts_listed = sb("ts_listed", [P, SLOTS], F32)
        ts_col, ts_square, ts_minus, upper, lower = [
            sb(name, [P, PACK], F32) for name in ("ts_col", "ts_square", "ts_minus", "upper", "lower")
        ]
        vector_copy(ts_listed[:], ts_row[:].indirect(offsets[:]))
        for t in range(PACK):
            nc.tensor.transpose(spare[1][:, t * P : (t + 1) * P], ts_listed[:, t::PACK], ident[:])
        scalar_copy(ts_col[:], spare[1][:, ::P])
        nc.vector.tensor_tensor(ts_square[:], ts_col[:], ts_col[:], ALU.mult)
        nc.vector.tensor_scalar(ts_minus[:], ts_col[:], -1.0, None, ALU.mult)
        nc.vector.tensor_tensor(upper[:], ts_col[:], ts_minus[:], ALU.max)
        nc.vector.tensor_tensor(lower[:], ts_col[:], ts_minus[:], ALU.min)

        listed = sb("listed", [P, PACK, SLOTS], BF16)
        stage = sb("stage", [P, PASS, PACK], BF16)
        wd_codes, wd_scales = sb("wd_codes", [P, SLOTS], U32), sb("wd_scales", [P, SLOTS], U8)
        ws_codes, ws_scales = sb("ws_codes", [P, D], U32), sb("ws_scales", [P, D], U8)
        x_codes = [sb("x_codes%d" % o, [P, PASS], U32) for o in range(GROUPS)]
        x_scales = [sb("x_scales%d" % o, [P, PASS], U8) for o in range(GROUPS)]
        y_scaled = [sb("y_scaled%d" % o, [P, PACK, PASS], F32) for o in range(GROUPS)]
        clipped = [sb("clipped%d" % o, [P, PACK, PASS], F32) for o in range(GROUPS)]
        result = [sb("result%d" % o, [P, PACK, D], F32) for o in range(GROUPS)]
        halves = [slice(0, PASS // 2), slice(PASS // 2, PASS)]

        def quantise(codes, scales, values, fmt):
            nc.vector.quantize_mx(codes.bitcast(fmt), scales, values.rearrange("p c t -> p (c t)"))

        def gather(t, first, last, engine_copy):
            window = table[t][:].indirect(offsets[:, first // LIST_ROWS : last // LIST_ROWS])
            engine_copy(listed[:, t, first:last], window)

        def scalar_gather(out, window):
            nc.scalar.activation(out, window, COPY)

        def interleave(engine_copy, out, planes):
            engine_copy(out.rearrange("p (c i) t -> p c t i", i=LINE), planes.rearrange("p t (c i) -> p c t i", i=LINE))

        def deal_w(n, engine_copy):
            engine_copy(
                stage[:, halves[n]].rearrange("p (s a b) t -> p a s b t", s=2, b=2),
                listed[:].rearrange("p t (a b s) -> p a s b t", b=2, s=PACK)[:, :, 2 * n : 2 * n + 2],
            )

        def turn_w(n):
            ws_in = sb("ws_in%d" % n, [P, D // 2, PACK], BF16)
            for k in range(2):
                words = listed[:, 2 * n + k, :].bitcast(F32)
                for u in range(2):
                    cols = slice((2 * k + u) * P, (2 * k + u + 1) * P)
                    nc.tensor.transpose(spare[n][:, cols], words[:, u::2], ident[:])
            scalar_copy(
                ws_in[:].rearrange("q d s -> q (d s)").bitcast(F32).rearrange("q (p ku) -> q p ku", ku=PACK),
                spare[n][:].rearrange("q (ku p) -> q p ku", ku=PACK),
            )
            quantise(ws_codes[:, halves[n]], ws_scales[:, halves[n]], ws_in[:], E4M3)

        def prepare_x(o, x_in):
            dealt = x_in[:].rearrange("p (e m) j -> p m j e", e=PACK)
            rows = x_raw[o][:].rearrange("p j (m e) -> p m j e", e=PACK)
            for ms in (slice(0, P // 2), slice(P // 2, P)):
                scalar_copy(dealt[:, ms], rows[:, ms])
            quantise(x_codes[o][:], x_scales[o][:], x_in[:], E4M3)

        def turn_y(o):
            for t in range(PACK):
                for e in range(PACK):
                    nc.tensor.transpose(quad[t][:, e * P : (e + 1) * P], y_raw[o][:, e, t::PACK], ident[:])
                nc.scalar.activation(y_scaled[o][:, t, :], quad[t][:], COPY, scale=ts_col[:, t : t + 1])

        def scores(o):
            diff = sb("diff%d" % o, [P, PACK, PASS], F32)
            for t in range(PACK):
                cols = slice(t * P, (t + 1) * P)
                nc.tensor.matmul_mx(
                    quad[t][:], wd_codes[:, cols].bitcast(E4M3), wd_scales[:, cols],
                    x_codes[o][:].bitcast(E4M3), x_scales[o][:], start=True, stop=True,
                )
                nc.vector.scalar_tensor_tensor(
                    diff[:, t, :], quad[t][:], ts_square[:, t : t + 1], y_scaled[o][:, t, :],
                    ALU.mult, ALU.subtract,
                )
            for t in range(PACK):
                engine = nc.gpsimd if t < GPSIMD_CLIPS else nc.vector
                engine.tensor_scalar(
                    clipped[o][:, t, :], diff[:, t, :], upper[:, t : t + 1], lower[:, t : t + 1], ALU.min, ALU.max
                )

        def gradient(o, pieces, out_banks, copies, tiles_a_store):
            h_in = sb("h_in%d" % o, [P, PASS, PACK], BF16)
            h_codes, h_scales = sb("h_codes%d" % o, [P, PASS], U32), sb("h_scales%d" % o, [P, PASS], U8)
            width = PASS // pieces
            parts = [slice(n * width, (n + 1) * width) for n in range(pieces)]

            def weigh(cols):
                weights = wt_banks[o][:, cols].rearrange("p (a i) -> p a i", i=2)
                nc.vector.tensor_tensor(
                    h_in[:, cols].rearrange("p (a i) t -> p a t i", i=2),
                    clipped[o][:, :, cols].rearrange("p t (a i) -> p a t i", i=2),
                    weights.unsqueeze(2).to_broadcast([P, width // 2, PACK, 2]),
                    ALU.mult,
                )

            def multiply(cols):
                quantise(h_codes[:, cols], h_scales[:, cols], h_in[:, cols], E5M2)
                for e in range(cols.start // P, cols.stop // P):
                    tile = slice(e * P, (e + 1) * P)
                    nc.tensor.matmul_mx(
                        out_banks[e][:], h_codes[:, tile].bitcast(E5M2), h_scales[:, tile],
                        ws_codes[:].bitcast(E4M3), ws_scales[:], start=True, stop=True,
                    )
                    copies[e](
                        result[o][:, e, :].rearrange("m (p n k) -> m p n k", n=2, k=2),
                        out_banks[e][:].rearrange("m (n p k) -> m p n k", n=2, k=2),
                    )
                    if (e + 1) % tiles_a_store == 0:
                        rows = slice(e + 1 - tiles_a_store, e + 1)
                        nc.sync.dma_start(out_view[o][:, rows, :], result[o][:, rows, :])

            weigh(parts[0])
            for done, coming in zip(parts, parts[1:]):
                weigh(coming)
                multiply(done)
            multiply(parts[-1])

        def round_result(o, shares):
            o_in = sb("o_in%d" % o, [P, D, PACK], BF16)
            for engine_copy, cols in shares:
                interleave(engine_copy, o_in[:, cols], result[o][:, :, cols])
            return o_in

        o_scales = sb("o_scales", [P, GROUPS, D], U8)

        def planes(o, o_in):
            o_codes = sb("o_codes%d" % o, [P, D], U32)
            quantise(o_codes[:], o_scales[:, o, :], o_in[:], E4M3)
            nc.sync.dma_start(out_1[o].rearrange("p d l -> p (d l)").bitcast(I32), o_codes[:].bitcast(I32))

        gather(0, 0, SLOTS, vector_copy)
        prepare_x(0, sb("x_first", [P, PASS, PACK], BF16))
        turn_y(0)
        gather(1, 0, SLOTS, vector_copy)
        turn_w(0)
        gather(2, 0, SLOTS, vector_copy)

        gather(3, 0, GATHER_CUT, vector_copy)
        gather(3, GATHER_CUT, SLOTS, scalar_gather)
        deal_w(0, vector_copy)
        deal_w(1, scalar_copy)
        for cols in halves:
            quantise(wd_codes[:, cols], wd_scales[:, cols], stage[:, cols], E4M3)

        scores(0)
        turn_w(1)
        prepare_x(1, stage)
        turn_y(1)
        gradient(0, 2, spare + spare, [scalar_copy] * PACK, 2)
        scores(1)
        first_rounded = round_result(0, [(scalar_copy, cols) for cols in halves])
        gradient(1, PACK, quad, [scalar_copy] * (PACK - 1) + [vector_copy], 1)
        planes(0, first_rounded)
        shares = [(vector_copy, slice(0, ROUND_CUT)), (scalar_copy, slice(ROUND_CUT, D))]
        planes(1, round_result(1, shares))
        for q, queue in enumerate((nc.scalar, nc.scalar, nc.sync, nc.sync)):
            scale_rows = out_2[:, 4 * q : 4 * q + 4, :].rearrange("o f d -> f o d")
            queue.dma_start(scale_rows.bitcast(I32), o_scales[32 * q : 32 * q + 4].bitcast(I32))
